import numpy as np
import ml_dtypes


def mxq(x, axis, fmt="e4m3"):
    dtype, down = {"e4m3": (ml_dtypes.float8_e4m3fn, 7), "e5m2": (ml_dtypes.float8_e5m2, 14)}[fmt]
    v = np.moveaxis(np.asarray(x, np.float32).astype(ml_dtypes.bfloat16).astype(np.float64), axis, -1)
    blocks = v.reshape(v.shape[:-1] + (-1, 32))
    amax = np.abs(blocks).max(-1, keepdims=True)
    byte = np.maximum(np.where(amax > 0, np.frexp(amax)[1] - 1 + 127, 0) - down, 1)
    scale = np.exp2(byte - 127.0)
    codes = (blocks / scale).astype(np.float32).astype(dtype).astype(np.float64)
    return np.moveaxis((codes * scale).reshape(v.shape), -1, axis)


WIDE = False


def mx_kscale(k):
    if not WIDE:
        return np.ones(k)
    levels = np.array([10, -10, 5, -5, 0])
    if k % 512:
        return np.exp2(np.random.permutation(np.resize(levels, k // 32))).repeat(32)
    a = np.empty((k // 512, 16))
    for p in range(k // 512):
        a[p, :8] = np.random.permutation(np.resize(levels, 8))
        for g in range(8):
            far = levels[np.abs(levels - a[p, g]) >= 10]
            a[p, g + 8] = far[np.random.randint(len(far))]
    return np.exp2(a.ravel()).repeat(32)


def f64(x):
    return np.asarray(x).astype(np.float64)


def striped(idx):
    return np.tile(idx.reshape(-1, 16).T, (8, 1)).astype(np.uint16)


def unstriped(offs):
    return offs[:16].T.reshape(-1).astype(np.int64)


E2M1 = np.array([0.0, 0.5, 1.0, 1.5, 2.0, 3.0, 4.0, 6.0, -0.0, -0.5, -1.0, -1.5, -2.0, -3.0, -4.0, -6.0])


def pack_weight(w, fmt):
    k, n = w.shape
    w = f64(np.asarray(w, np.float32).astype(ml_dtypes.bfloat16)).reshape(k // 32, 32, n)
    amax = np.abs(w).max(1)
    if fmt == "e4m3":
        byte = np.frexp(amax)[1] - 1 + 127 - 7
    else:
        mant, ex = np.frexp(amax / 6.0)
        byte = np.where(mant > 0.5, ex, ex - 1) + 127
    byte = np.clip(np.where(amax > 0, byte, 1), 1, 254)
    scaled = (w * np.exp2(127.0 - byte)[:, None, :]).reshape(k, n).astype(np.float32)
    by_word = np.ascontiguousarray(scaled.reshape(k // 512, 128, 4, n).transpose(0, 1, 3, 2))
    if fmt == "e4m3":
        words = by_word.astype(ml_dtypes.float8_e4m3fn).view(np.uint8)
    else:
        c = by_word.astype(ml_dtypes.float4_e2m1fn).view(np.uint8) & 0xF
        words = (c[..., 0::2] | (c[..., 1::2] << 4)).reshape(k // 512, 128, 2 * n)
    return np.ascontiguousarray(words), np.ascontiguousarray(byte.astype(np.uint8).reshape(k // 512, 16, n))


def unpack_weight(words, scales, fmt):
    g, _, n = scales.shape
    words = np.ascontiguousarray(words).reshape(g, 128, n, -1)
    if fmt == "e4m3":
        vals = words.view(ml_dtypes.float8_e4m3fn).astype(np.float64)
    else:
        nib = np.empty((g, 128, n, 4), np.uint8)
        nib[..., 0::2] = words & 0xF
        nib[..., 1::2] = words >> 4
        vals = E2M1[nib]
    vals = vals * np.repeat(np.exp2(scales.astype(np.float64) - 127.0), 8, axis=1)[..., None]
    return vals.transpose(0, 1, 3, 2).reshape(g * 512, n)


def gelu(v):
    return 0.5 * v * (1.0 + np.tanh(np.sqrt(2.0 / np.pi) * (v + 0.044715 * v**3)))


K, T, E, C, N = 2048, 1024, 12, 256, 128
TOP = 3


def by_expert(wq, xq):
    return np.concatenate([wq[e].T @ xq[:, e * C:(e + 1) * C] for e in range(E)], axis=1)


def setup_inputs():
    n = np.random.standard_normal
    s = mx_kscale(K)[:, None]
    deal = np.repeat(np.arange(E), C).reshape(TOP, T)[:, np.random.permutation(T)]
    deal = np.take_along_axis(deal, np.argsort(np.random.rand(TOP, T), axis=0), axis=0)
    for _ in range(8):
        s_, t_ = np.random.permutation(T).reshape(2, -1); r = np.random.randint(TOP, size=T // 2); x, y = deal[r, s_].copy(), deal[r, t_].copy()
        ok = ~((deal[:, s_] == y).any(0) | (deal[:, t_] == x).any(0)); deal[r[ok], s_[ok]] = y[ok]; deal[r[ok], t_[ok]] = x[ok]
    order = np.lexsort((np.random.rand(TOP * T), deal.reshape(-1)))
    slot_token = order % T; pos = np.empty(TOP * T, np.int64); pos[order] = np.arange(TOP * T); pos = pos.reshape(TOP, T)
    g = np.random.uniform(0.5, 1.5, (TOP, T)); g = g / g.sum(0)
    w = [pack_weight(m, "e2m1") for m in n((E, K, N)) / np.sqrt(K) / s[None]]
    return {
        "xT": (n((K, T)) * s).astype(np.float32),
        "w_words": np.stack([m[0] for m in w]),
        "w_scales": np.stack([m[1] for m in w]),
        "b": (0.3 * n((N, E))).astype(np.float32),
        "gate": np.stack([np.tile(r, (N, 1)) for r in g]).astype(np.float32),
        "offs": striped(slot_token),
        "pos1": striped(pos[0]),
        "pos2": striped(pos[1]),
        "pos3": striped(pos[2]),
    }


def reference(xT, w_words, w_scales, b, gate, offs, pos1, pos2, pos3):
    idx = unstriped(offs)
    w = np.stack([unpack_weight(w_words[e], w_scales[e], "e2m1") for e in range(E)])
    xq = mxq(f64(xT)[:, idx], 0, "e4m3")
    y = by_expert(w, xq)
    y = gelu(y + np.repeat(f64(b), C, axis=1))
    return sum(f64(gate[r]) * y[:, unstriped(p)] for r, p in enumerate((pos1, pos2, pos3)))

@@ -1,0 +1,206 @@
+from contextlib import ExitStack
+
+import concourse.mybir as mybir
+
+K, T, E, C, N = 2048, 1024, 12, 256, 128
+TOP = 3
+S = E * C
+P = 128
+PACK = 4
+K_PASS = P * PACK
+PASSES = K // K_PASS
+FLOPS = 2 * K * N * S
+
+F32 = mybir.dt.float32
+BF16 = mybir.dt.bfloat16
+I32 = mybir.dt.int32
+U32 = mybir.dt.uint32
+U16 = mybir.dt.uint16
+U8 = mybir.dt.uint8
+FP8X4 = mybir.dt.float8_e4m3fn_x4
+FP4X4 = mybir.dt.float4_e2m1fn_x4
+AF = mybir.ActivationFunctionType
+MULT = mybir.AluOpType.mult
+ADD = mybir.AluOpType.add
+
+GROUP = 128
+LIST = 16
+
+
+def tile_moe_tk_lin_gelu_kernel(tc, xT, w_words, w_scales, b, gate, offs, pos1, pos2, pos3, out):
+    nc = tc.nc
+    with ExitStack() as ctx:
+        keep = ctx.enter_context(tc.tile_pool(name="keep", bufs=1))
+        raws = ctx.enter_context(tc.tile_pool(name="raws", bufs=5))
+        stage = ctx.enter_context(tc.tile_pool(name="stage", bufs=4))
+        prods = ctx.enter_context(tc.tile_pool(name="prods", bufs=4))
+        psum = ctx.enter_context(tc.psum_pool(name="psum", bufs=8))
+
+        offs_t = keep.tile([P, S // LIST], U16, name="offs_t")
+        pos_t = [keep.tile([P, T // LIST], U16, name="pos%d_t" % r) for r in range(TOP)]
+        x_scales = keep.tile([P, T], U8, name="x_scales", align_bytes=64)
+        codes = [keep.tile([P, T], U32, name="codes%d" % a, align_bytes=64) for a in range(PASSES)]
+        slot_codes = [keep.tile([P, S], U32, name="slot_codes%d" % a, align_bytes=64) for a in range(PASSES)]
+        slot_scales = [keep.tile([P, S], U8, name="slot_scales%d" % a, align_bytes=64) for a in range(PASSES)]
+        w_codes = keep.tile([P, E * PASSES, 2 * N], U8, name="w_codes", align_bytes=64)
+        w_planes = keep.tile([P, E * PASSES, N], U8, name="w_planes", align_bytes=64)
+        b_t = keep.tile([P, E], F32, name="b_t")
+        gate_t = [keep.tile([P, T], F32, name="gate%d" % r) for r in range(TOP)]
+        y = keep.tile([P, S], F32, name="y")
+        warm = keep.tile([P, 1], F32, name="warm")
+        warm_out = keep.tile([P, 1], F32, name="warm_out")
+
+        nc.vector.memset(warm[:], 0.0)
+        nc.scalar.activation(out=warm_out[:], in_=warm[:], func=AF.Gelu_apprx_tanh)
+        nc.gpsimd.memset(x_scales[:].bitcast(I32), 0)
+        nc.gpsimd.memset(w_planes[:].rearrange("p g n -> p (g n)").bitcast(I32), 0)
+        for a in range(1, PASSES):
+            nc.gpsimd.memset(slot_scales[a][:].bitcast(I32), 0)
+
+        def load_x(a, c0, width):
+            raw = raws.tile([P, PACK, width], F32, name="raw")
+            rows = xT[a * K_PASS:(a + 1) * K_PASS, c0:c0 + width]
+            nc.sync.dma_start(raw[:], rows.rearrange("(p j) w -> p j w", j=PACK))
+            return raw
+
+        pieces = {}
+        first = ((0, 256), (256, 256), (512, 256), (768, 128), (896, 128))
+        for c0, width in first:
+            pieces[(0, c0)] = (load_x(0, c0, width), width)
+            if c0 == 256:
+                nc.sync.dma_start(offs_t[:], offs)
+        for a in range(1, PASSES):
+            for c0 in range(0, T, 512):
+                pieces[(a, c0)] = (load_x(a, c0, 512), 512)
+        for e0 in range(0, E, 3):
+            nc.sync.dma_start(
+                w_codes[:, e0 * PASSES:(e0 + 3) * PASSES, :].bitcast(I32),
+                w_words[e0:e0 + 3].rearrange("e a p n -> p (e a) n").bitcast(I32),
+            )
+        for r in range(4):
+            nc.sync.dma_start(
+                w_planes[r:P:32, :, :].bitcast(I32),
+                w_scales.rearrange("e a (q r) n -> r q (e a) n", r=4)[r].bitcast(I32),
+            )
+        nc.sync.dma_start(b_t[:], b)
+        for r, pos in enumerate((pos1, pos2, pos3)):
+            nc.sync.dma_start(pos_t[r][:], pos)
+            nc.sync.dma_start(gate_t[r][:], gate[r])
+
+        def interleave(a, c0, on_vector):
+            raw, width = pieces[(a, c0)]
+            grouped = stage.tile([P, width, PACK], BF16, name="grouped", align_bytes=64)
+            src = raw[:].rearrange("p j w -> p w j")
+            if on_vector:
+                nc.vector.tensor_copy(out=grouped[:], in_=src)
+            else:
+                nc.scalar.copy(out=grouped[:], in_=src)
+            return grouped
+
+        def quantize(a, c0, grouped):
+            width = pieces[(a, c0)][1]
+            nc.vector.quantize_mx(
+                out=codes[a][:, c0:c0 + width].bitcast(FP8X4),
+                scales=x_scales[4 * a:P, c0:c0 + width],
+                in_=grouped[:].rearrange("p w j -> p (w j)"),
+            )
+
+        def gather_codes(a, s0, n):
+            nc.vector.tensor_copy(
+                out=slot_codes[a][:, s0:s0 + n],
+                in_=codes[a][:].indirect(offs_t[:, s0 // LIST:(s0 + n) // LIST]),
+            )
+
+        def gather_scales(s0, n):
+            nc.vector.tensor_copy(
+                out=slot_scales[0][:, s0:s0 + n],
+                in_=x_scales[:].indirect(offs_t[:, s0 // LIST:(s0 + n) // LIST]),
+            )
+
+        for c0, width in first:
+            quantize(0, c0, interleave(0, c0, True))
+        for s0 in range(0, S, 768):
+            gather_codes(0, s0, 768)
+        for c0 in range(0, T, 512):
+            quantize(1, c0, interleave(1, c0, False))
+        for s0 in range(0, S, 768):
+            gather_codes(1, s0, 768)
+        for c0 in range(0, T, 512):
+            quantize(2, c0, interleave(2, c0, False))
+        gather_codes(2, 0, 768)
+        for c0 in range(0, T, 512):
+            quantize(3, c0, interleave(3, c0, False))
+        for s0 in range(0, S, 768):
+            gather_scales(s0, 768)
+        for a in range(1, PASSES):
+            for r in range(4):
+                nc.sync.dma_start(
+                    slot_scales[a][r:P:32, :].bitcast(I32),
+                    slot_scales[0][4 * a + r:P:32, :].bitcast(I32),
+                )
+
+        acc = {}
+
+        def multiply(g, a):
+            s0, e = g * GROUP, g * GROUP // C
+            if a == 0:
+                acc[g] = psum.tile([P, GROUP], F32, name="acc")
+            nc.tensor.matmul_mx(
+                out=acc[g][:],
+                lhsT=w_codes[:, e * PASSES + a, :].bitcast(FP4X4),
+                lhsT_scale=w_planes[:, e * PASSES + a, :],
+                rhs=slot_codes[a][:, s0:s0 + GROUP].bitcast(FP8X4),
+                rhs_scale=slot_scales[a][:, s0:s0 + GROUP],
+                start=(a == 0),
+                stop=(a == PASSES - 1),
+            )
+
+        groups = S // GROUP
+        for g in range(6):
+            for a in range(PASSES - 1):
+                multiply(g, a)
+        done = 0
+        for n in (768, 768, 768, 640, 128):
+            if done and done % 768 == 0:
+                gather_codes(2, done, 768)
+                for g in range(done // GROUP, done // GROUP + 6):
+                    for a in range(PASSES - 1):
+                        multiply(g, a)
+            gather_codes(3, done, n)
+            for g in range(done // GROUP, (done + n) // GROUP):
+                multiply(g, PASSES - 1)
+                e = g * GROUP // C
+                nc.scalar.activation(
+                    out=y[:, g * GROUP:(g + 1) * GROUP], in_=acc[g][:],
+                    func=AF.Gelu_apprx_tanh, bias=b_t[:, e:e + 1],
+                )
+            done += n
+
+        bounds = (0, 576, T)
+        prod = {}
+
+        def pick(h, r):
+            t0, t1 = bounds[h], bounds[h + 1]
+            prod[(h, r)] = prods.tile([P, t1 - t0], F32, name="prod%d" % r)
+            nc.vector.tensor_tensor(
+                prod[(h, r)][:], y[:].indirect(pos_t[r][:, t0 // LIST:t1 // LIST]), gate_t[r][:, t0:t1], MULT,
+            )
+
+        def add(h, r, c0, c1):
+            nc.vector.tensor_tensor(prod[(h, 0)][:, c0:c1], prod[(h, 0)][:, c0:c1], prod[(h, r)][:, c0:c1], ADD)
+
+        first_width, last_width = bounds[1], T - bounds[1]
+        for r in range(TOP):
+            pick(0, r)
+        add(0, 1, 0, first_width)
+        pick(1, 0)
+        add(0, 2, 0, first_width)
+        nc.sync.dma_start(out[:, 0:first_width], prod[(0, 0)][:])
+        pick(1, 1)
+        pick(1, 2)
+        cuts = ((0, last_width // 2), (last_width // 2, last_width))
+        for c0, c1 in cuts:
+            add(1, 1, c0, c1)
+        for c0, c1 in cuts:
+            add(1, 2, c0, c1)
+            nc.sync.dma_start(out[:, first_width + c0:first_width + c1], prod[(1, 0)][:, c0:c1])

@@ -33,13 +33,13 @@ def tile_moe_tk_lin_gelu_kernel(tc, xT, w_words, w_scales, b, gate, offs, pos1, 
         keep = ctx.enter_context(tc.tile_pool(name="keep", bufs=1))
         raws = ctx.enter_context(tc.tile_pool(name="raws", bufs=5))
         stage = ctx.enter_context(tc.tile_pool(name="stage", bufs=4))
-        prods = ctx.enter_context(tc.tile_pool(name="prods", bufs=4))
+        prods = ctx.enter_context(tc.tile_pool(name="prods", bufs=1))
         psum = ctx.enter_context(tc.psum_pool(name="psum", bufs=8))
 
         offs_t = keep.tile([P, S // LIST], U16, name="offs_t")
         pos_t = [keep.tile([P, T // LIST], U16, name="pos%d_t" % r) for r in range(TOP)]
-        x_scales = keep.tile([P, T], U8, name="x_scales", align_bytes=64)
-        codes = [keep.tile([P, T], U32, name="codes%d" % a, align_bytes=64) for a in range(PASSES)]
+        x_scales = keep.tile([P, 2 * T], U8, name="x_scales", align_bytes=64)
+        codes = keep.tile([P, (PASSES + 1) * T], I32, name="codes", align_bytes=64)
         slot_codes = [keep.tile([P, S], U32, name="slot_codes%d" % a, align_bytes=64) for a in range(PASSES)]
         slot_scales = [keep.tile([P, S], U8, name="slot_scales%d" % a, align_bytes=64) for a in range(PASSES)]
         w_codes = keep.tile([P, E * PASSES, 2 * N], U8, name="w_codes", align_bytes=64)
@@ -51,6 +51,7 @@ def tile_moe_tk_lin_gelu_kernel(tc, xT, w_words, w_scales, b, gate, offs, pos1, 
         warm_out = keep.tile([P, 1], F32, name="warm_out")
 
         nc.vector.memset(warm[:], 0.0)
+        nc.vector.memset(codes[:, PASSES * T:], 0)
         nc.scalar.activation(out=warm_out[:], in_=warm[:], func=AF.Gelu_apprx_tanh)
         nc.gpsimd.memset(x_scales[:].bitcast(I32), 0)
         nc.gpsimd.memset(w_planes[:].rearrange("p g n -> p (g n)").bitcast(I32), 0)
@@ -64,51 +65,53 @@ def tile_moe_tk_lin_gelu_kernel(tc, xT, w_words, w_scales, b, gate, offs, pos1, 
             return raw
 
         pieces = {}
-        first = ((0, 256), (256, 256), (512, 256), (768, 128), (896, 128))
-        for c0, width in first:
-            pieces[(0, c0)] = (load_x(0, c0, width), width)
-            if c0 == 256:
-                nc.sync.dma_start(offs_t[:], offs)
-        for a in range(1, PASSES):
-            for c0 in range(0, T, 512):
-                pieces[(a, c0)] = (load_x(a, c0, 512), 512)
-        for e0 in range(0, E, 3):
+
+        def load_pass(a, widths):
+            c0 = 0
+            for width in widths:
+                pieces[(a, c0)] = (load_x(a, c0, width), width)
+                c0 += width
+
+        def load_w(e0, e1):
             nc.sync.dma_start(
-                w_codes[:, e0 * PASSES:(e0 + 3) * PASSES, :].bitcast(I32),
-                w_words[e0:e0 + 3].rearrange("e a p n -> p (e a) n").bitcast(I32),
+                w_codes[:, e0 * PASSES:e1 * PASSES, :].bitcast(I32),
+                w_words[e0:e1].rearrange("e a p n -> p (e a) n").bitcast(I32),
             )
+
+        load_pass(0, (256, 256, 256, 128, 128))
+        nc.sync.dma_start(offs_t[:], offs)
+        load_pass(1, (512, 512))
+        load_pass(2, (512, 512))
+        load_pass(3, (512, 512))
+        load_w(0, 3)
         for r in range(4):
             nc.sync.dma_start(
                 w_planes[r:P:32, :, :].bitcast(I32),
                 w_scales.rearrange("e a (q r) n -> r q (e a) n", r=4)[r].bitcast(I32),
             )
+        for e0 in (3, 6, 9):
+            load_w(e0, e0 + 3)
         nc.sync.dma_start(b_t[:], b)
-        for r, pos in enumerate((pos1, pos2, pos3)):
-            nc.sync.dma_start(pos_t[r][:], pos)
-            nc.sync.dma_start(gate_t[r][:], gate[r])
 
-        def interleave(a, c0, on_vector):
-            raw, width = pieces[(a, c0)]
+        def quantize(a, key, lo, hi, on_vector):
+            raw = pieces[(a, key)][0]
+            width = hi - lo
             grouped = stage.tile([P, width, PACK], BF16, name="grouped", align_bytes=64)
-            src = raw[:].rearrange("p j w -> p w j")
+            src = raw[:, :, lo - key:hi - key].rearrange("p j w -> p w j")
             if on_vector:
                 nc.vector.tensor_copy(out=grouped[:], in_=src)
             else:
                 nc.scalar.copy(out=grouped[:], in_=src)
-            return grouped
-
-        def quantize(a, c0, grouped):
-            width = pieces[(a, c0)][1]
-            nc.vector.quantize_mx(
-                out=codes[a][:, c0:c0 + width].bitcast(FP8X4),
-                scales=x_scales[4 * a:P, c0:c0 + width],
+            return lambda: nc.vector.quantize_mx(
+                out=codes[:, (PASSES - 1 - a) * T + lo:(PASSES - 1 - a) * T + hi].bitcast(FP8X4),
+                scales=x_scales[4 * a:P, lo:hi],
                 in_=grouped[:].rearrange("p w j -> p (w j)"),
             )
 
         def gather_codes(a, s0, n):
             nc.vector.tensor_copy(
                 out=slot_codes[a][:, s0:s0 + n],
-                in_=codes[a][:].indirect(offs_t[:, s0 // LIST:(s0 + n) // LIST]),
+                in_=codes[:, (PASSES - 1 - a) * T:(PASSES - 1 - a) * T + (2 * T if n > 768 else T)].bitcast(U32).indirect(offs_t[:, s0 // LIST:(s0 + n) // LIST]),
             )
 
         def gather_scales(s0, n):
@@ -117,27 +120,30 @@ def tile_moe_tk_lin_gelu_kernel(tc, xT, w_words, w_scales, b, gate, offs, pos1, 
                 in_=x_scales[:].indirect(offs_t[:, s0 // LIST:(s0 + n) // LIST]),
             )
 
-        for c0, width in first:
-            quantize(0, c0, interleave(0, c0, True))
-        for s0 in range(0, S, 768):
-            gather_codes(0, s0, 768)
-        for c0 in range(0, T, 512):
-            quantize(1, c0, interleave(1, c0, False))
-        for s0 in range(0, S, 768):
-            gather_codes(1, s0, 768)
-        for c0 in range(0, T, 512):
-            quantize(2, c0, interleave(2, c0, False))
-        gather_codes(2, 0, 768)
-        for c0 in range(0, T, 512):
-            quantize(3, c0, interleave(3, c0, False))
-        for s0 in range(0, S, 768):
-            gather_scales(s0, 768)
-        for a in range(1, PASSES):
-            for r in range(4):
+        def gather_and_move_scales(s0, s1):
+            gather_scales(s0, s1 - s0)
+            for a in range(1, PASSES):
                 nc.sync.dma_start(
-                    slot_scales[a][r:P:32, :].bitcast(I32),
-                    slot_scales[0][4 * a + r:P:32, :].bitcast(I32),
+                    slot_scales[a][0:112, s0:s1].bitcast(I32),
+                    slot_scales[0][4 * a:4 * a + 112, s0:s1].bitcast(I32),
                 )
+
+        for c0, width in ((0, 256), (256, 256), (512, 256), (768, 128), (896, 128)):
+            quantize(0, c0, c0, c0 + width, True)()
+        for s0 in (0, 1536):
+            gather_codes(0, s0, 1536)
+        for c0 in (0, 512):
+            quantize(1, c0, c0, c0 + 512, False)()
+        for s0 in (0, 1536):
+            gather_codes(1, s0, 1536)
+        for c0 in (0, 512):
+            quantize(2, c0, c0, c0 + 512, False)()
+        for c0 in (0, 512):
+            quantize(3, c0, c0, c0 + 512, False)()
+        gather_and_move_scales(0, 1536)
+        for r, pos in enumerate((pos1, pos2, pos3)):
+            nc.sync.dma_start(pos_t[r][:], pos)
+            nc.sync.dma_start(gate_t[r][:], gate[r])
 
         acc = {}
 
@@ -155,52 +161,47 @@ def tile_moe_tk_lin_gelu_kernel(tc, xT, w_words, w_scales, b, gate, offs, pos1, 
                 stop=(a == PASSES - 1),
             )
 
-        groups = S // GROUP
-        for g in range(6):
-            for a in range(PASSES - 1):
-                multiply(g, a)
-        done = 0
-        for n in (768, 768, 768, 640, 128):
-            if done and done % 768 == 0:
-                gather_codes(2, done, 768)
-                for g in range(done // GROUP, done // GROUP + 6):
-                    for a in range(PASSES - 1):
-                        multiply(g, a)
-            gather_codes(3, done, n)
-            for g in range(done // GROUP, (done + n) // GROUP):
+        def open_groups(s0, s1):
+            for g in range(s0 // GROUP, s1 // GROUP):
+                for a in range(PASSES - 1):
+                    multiply(g, a)
+
+        def close_groups(s0, s1):
+            for g in range(s0 // GROUP, s1 // GROUP):
                 multiply(g, PASSES - 1)
                 e = g * GROUP // C
                 nc.scalar.activation(
                     out=y[:, g * GROUP:(g + 1) * GROUP], in_=acc[g][:],
                     func=AF.Gelu_apprx_tanh, bias=b_t[:, e:e + 1],
                 )
-            done += n
 
-        bounds = (0, 576, T)
-        prod = {}
+        for s0 in range(0, S, 768):
+            gather_codes(2, s0, 768)
+            open_groups(s0, s0 + 768)
+            sizes = (768,) if s0 + 768 < S else (640, 128)
+            lo = s0
+            for n in sizes:
+                gather_codes(3, lo, n)
+                close_groups(lo, lo + n)
+                lo += n
+            if s0 == 768:
+                gather_and_move_scales(1536, S)
 
-        def pick(h, r):
-            t0, t1 = bounds[h], bounds[h + 1]
-            prod[(h, r)] = prods.tile([P, t1 - t0], F32, name="prod%d" % r)
+        prod = [prods.tile([P, T], F32, name="prod%d" % r) for r in range(TOP)]
+
+        def pick(r, t0, t1):
             nc.vector.tensor_tensor(
-                prod[(h, r)][:], y[:].indirect(pos_t[r][:, t0 // LIST:t1 // LIST]), gate_t[r][:, t0:t1], MULT,
+                prod[r][:, t0:t1], y[:].indirect(pos_t[r][:, t0 // LIST:t1 // LIST]), gate_t[r][:, t0:t1], MULT,
             )
 
-        def add(h, r, c0, c1):
-            nc.vector.tensor_tensor(prod[(h, 0)][:, c0:c1], prod[(h, 0)][:, c0:c1], prod[(h, r)][:, c0:c1], ADD)
+        def add(r, t0, t1):
+            nc.vector.tensor_tensor(prod[0][:, t0:t1], prod[0][:, t0:t1], prod[r][:, t0:t1], ADD)
 
-        first_width, last_width = bounds[1], T - bounds[1]
-        for r in range(TOP):
-            pick(0, r)
-        add(0, 1, 0, first_width)
-        pick(1, 0)
-        add(0, 2, 0, first_width)
-        nc.sync.dma_start(out[:, 0:first_width], prod[(0, 0)][:])
-        pick(1, 1)
-        pick(1, 2)
-        cuts = ((0, last_width // 2), (last_width // 2, last_width))
-        for c0, c1 in cuts:
-            add(1, 1, c0, c1)
-        for c0, c1 in cuts:
-            add(1, 2, c0, c1)
-            nc.sync.dma_start(out[:, first_width + c0:first_width + c1], prod[(1, 0)][:, c0:c1])
+        pick(0, 0, T)
+        pick(1, 0, T)
+        pick(2, 0, 576)
+        add(1, 0, T)
+        pick(2, 576, T)
+        for t0, t1 in ((0, 576), (576, 800), (800, T)):
+            add(2, t0, t1)
+            nc.sync.dma_start(out[:, t0:t1], prod[0][:, t0:t1])

@@ -31,15 +31,15 @@ def tile_moe_tk_lin_gelu_kernel(tc, xT, w_words, w_scales, b, gate, offs, pos1, 
     nc = tc.nc
     with ExitStack() as ctx:
         keep = ctx.enter_context(tc.tile_pool(name="keep", bufs=1))
-        raws = ctx.enter_context(tc.tile_pool(name="raws", bufs=5))
+        raws = ctx.enter_context(tc.tile_pool(name="raws", bufs=1))
         stage = ctx.enter_context(tc.tile_pool(name="stage", bufs=4))
         prods = ctx.enter_context(tc.tile_pool(name="prods", bufs=1))
         psum = ctx.enter_context(tc.psum_pool(name="psum", bufs=8))
 
         offs_t = keep.tile([P, S // LIST], U16, name="offs_t")
         pos_t = [keep.tile([P, T // LIST], U16, name="pos%d_t" % r) for r in range(TOP)]
-        x_scales = keep.tile([P, 2 * T], U8, name="x_scales", align_bytes=64)
-        codes = keep.tile([P, (PASSES + 1) * T], I32, name="codes", align_bytes=64)
+        x_scales = keep.tile([P, T], U8, name="x_scales", align_bytes=64)
+        codes = [keep.tile([P, T], U32, name="codes%d" % a, align_bytes=64) for a in range(PASSES)]
         slot_codes = [keep.tile([P, S], U32, name="slot_codes%d" % a, align_bytes=64) for a in range(PASSES)]
         slot_scales = [keep.tile([P, S], U8, name="slot_scales%d" % a, align_bytes=64) for a in range(PASSES)]
         w_codes = keep.tile([P, E * PASSES, 2 * N], U8, name="w_codes", align_bytes=64)
@@ -51,15 +51,14 @@ def tile_moe_tk_lin_gelu_kernel(tc, xT, w_words, w_scales, b, gate, offs, pos1, 
         warm_out = keep.tile([P, 1], F32, name="warm_out")
 
         nc.vector.memset(warm[:], 0.0)
-        nc.vector.memset(codes[:, PASSES * T:], 0)
         nc.scalar.activation(out=warm_out[:], in_=warm[:], func=AF.Gelu_apprx_tanh)
         nc.gpsimd.memset(x_scales[:].bitcast(I32), 0)
-        nc.gpsimd.memset(w_planes[:].rearrange("p g n -> p (g n)").bitcast(I32), 0)
+        nc.vector.memset(w_planes[:].rearrange("p g n -> p (g n)").bitcast(I32), 0)
         for a in range(1, PASSES):
-            nc.gpsimd.memset(slot_scales[a][:].bitcast(I32), 0)
+            nc.vector.memset(slot_scales[a][:].bitcast(I32), 0)
 
         def load_x(a, c0, width):
-            raw = raws.tile([P, PACK, width], F32, name="raw")
+            raw = raws.tile([P, PACK, width], F32, name="raw%d_%d" % (a, c0))
             rows = xT[a * K_PASS:(a + 1) * K_PASS, c0:c0 + width]
             nc.sync.dma_start(raw[:], rows.rearrange("(p j) w -> p j w", j=PACK))
             return raw
@@ -82,14 +81,13 @@ def tile_moe_tk_lin_gelu_kernel(tc, xT, w_words, w_scales, b, gate, offs, pos1, 
         nc.sync.dma_start(offs_t[:], offs)
         load_pass(1, (512, 512))
         load_pass(2, (512, 512))
-        load_pass(3, (512, 512))
-        load_w(0, 3)
+        load_pass(3, (512, 256, 256))
         for r in range(4):
             nc.sync.dma_start(
                 w_planes[r:P:32, :, :].bitcast(I32),
                 w_scales.rearrange("e a (q r) n -> r q (e a) n", r=4)[r].bitcast(I32),
             )
-        for e0 in (3, 6, 9):
+        for e0 in range(0, E, 3):
             load_w(e0, e0 + 3)
         nc.sync.dma_start(b_t[:], b)
 
@@ -97,13 +95,14 @@ def tile_moe_tk_lin_gelu_kernel(tc, xT, w_words, w_scales, b, gate, offs, pos1, 
             raw = pieces[(a, key)][0]
             width = hi - lo
             grouped = stage.tile([P, width, PACK], BF16, name="grouped", align_bytes=64)
-            src = raw[:, :, lo - key:hi - key].rearrange("p j w -> p w j")
+            src = raw[:, :, lo - key:hi - key].rearrange("p j (c i) -> p c j i", i=4)
+            dst = grouped[:].rearrange("p (c i) j -> p c j i", i=4)
             if on_vector:
-                nc.vector.tensor_copy(out=grouped[:], in_=src)
+                nc.vector.tensor_copy(out=dst, in_=src)
             else:
-                nc.scalar.copy(out=grouped[:], in_=src)
+                nc.scalar.copy(out=dst, in_=src)
             return lambda: nc.vector.quantize_mx(
-                out=codes[:, (PASSES - 1 - a) * T + lo:(PASSES - 1 - a) * T + hi].bitcast(FP8X4),
+                out=codes[a][:, lo:hi].bitcast(FP8X4),
                 scales=x_scales[4 * a:P, lo:hi],
                 in_=grouped[:].rearrange("p w j -> p (w j)"),
             )
@@ -111,7 +110,7 @@ def tile_moe_tk_lin_gelu_kernel(tc, xT, w_words, w_scales, b, gate, offs, pos1, 
         def gather_codes(a, s0, n):
             nc.vector.tensor_copy(
                 out=slot_codes[a][:, s0:s0 + n],
-                in_=codes[:, (PASSES - 1 - a) * T:(PASSES - 1 - a) * T + (2 * T if n > 768 else T)].bitcast(U32).indirect(offs_t[:, s0 // LIST:(s0 + n) // LIST]),
+                in_=codes[a][:].indirect(offs_t[:, s0 // LIST:(s0 + n) // LIST]),
             )
 
         def gather_scales(s0, n):
@@ -121,7 +120,8 @@ def tile_moe_tk_lin_gelu_kernel(tc, xT, w_words, w_scales, b, gate, offs, pos1, 
             )
 
         def gather_and_move_scales(s0, s1):
-            gather_scales(s0, s1 - s0)
+            for lo in range(s0, s1, 768):
+                gather_scales(lo, 768)
             for a in range(1, PASSES):
                 nc.sync.dma_start(
                     slot_scales[a][0:112, s0:s1].bitcast(I32),
@@ -130,17 +130,18 @@ def tile_moe_tk_lin_gelu_kernel(tc, xT, w_words, w_scales, b, gate, offs, pos1, 
 
         for c0, width in ((0, 256), (256, 256), (512, 256), (768, 128), (896, 128)):
             quantize(0, c0, c0, c0 + width, True)()
-        for s0 in (0, 1536):
-            gather_codes(0, s0, 1536)
+        for s0 in range(0, S, 768):
+            gather_codes(0, s0, 768)
         for c0 in (0, 512):
             quantize(1, c0, c0, c0 + 512, False)()
-        for s0 in (0, 1536):
-            gather_codes(1, s0, 1536)
+        for s0 in (0, 768):
+            gather_codes(1, s0, 768)
         for c0 in (0, 512):
             quantize(2, c0, c0, c0 + 512, False)()
-        for c0 in (0, 512):
-            quantize(3, c0, c0, c0 + 512, False)()
+        for c0, width in ((0, 512), (512, 256), (768, 256)):
+            quantize(3, c0, c0, c0 + width, False)()
         gather_and_move_scales(0, 1536)
+        gather_and_move_scales(1536, S)
         for r, pos in enumerate((pos1, pos2, pos3)):
             nc.sync.dma_start(pos_t[r][:], pos)
             nc.sync.dma_start(gate_t[r][:], gate[r])
@@ -162,8 +163,8 @@ def tile_moe_tk_lin_gelu_kernel(tc, xT, w_words, w_scales, b, gate, offs, pos1, 
             )
 
         def open_groups(s0, s1):
-            for g in range(s0 // GROUP, s1 // GROUP):
-                for a in range(PASSES - 1):
+            for a in range(PASSES - 1):
+                for g in range(s0 // GROUP, s1 // GROUP):
                     multiply(g, a)
 
         def close_groups(s0, s1):
@@ -176,6 +177,8 @@ def tile_moe_tk_lin_gelu_kernel(tc, xT, w_words, w_scales, b, gate, offs, pos1, 
                 )
 
         for s0 in range(0, S, 768):
+            if s0 >= 1536:
+                gather_codes(1, s0, 768)
             gather_codes(2, s0, 768)
             open_groups(s0, s0 + 768)
             sizes = (768,) if s0 + 768 < S else (640, 128)
@@ -184,8 +187,6 @@ def tile_moe_tk_lin_gelu_kernel(tc, xT, w_words, w_scales, b, gate, offs, pos1, 
                 gather_codes(3, lo, n)
                 close_groups(lo, lo + n)
                 lo += n
-            if s0 == 768:
-                gather_and_move_scales(1536, S)
 
         prod = [prods.tile([P, T], F32, name="prod%d" % r) for r in range(TOP)]
 

@@ -39,7 +39,8 @@ def tile_moe_tk_lin_gelu_kernel(tc, xT, w_words, w_scales, b, gate, offs, pos1, 
         offs_t = keep.tile([P, S // LIST], U16, name="offs_t")
         pos_t = [keep.tile([P, T // LIST], U16, name="pos%d_t" % r) for r in range(TOP)]
         x_scales = keep.tile([P, T], U8, name="x_scales", align_bytes=64)
-        codes = [keep.tile([P, T], U32, name="codes%d" % a, align_bytes=64) for a in range(PASSES)]
+        codes = [keep.tile([P, T], U32, name="codes%d" % a, align_bytes=64) for a in range(2)]
+        late_codes = keep.tile([P, 2 * T], U32, name="late_codes", align_bytes=64)
         slot_codes = [keep.tile([P, S], U32, name="slot_codes%d" % a, align_bytes=64) for a in range(PASSES)]
         slot_scales = [keep.tile([P, S], U8, name="slot_scales%d" % a, align_bytes=64) for a in range(PASSES)]
         w_codes = keep.tile([P, E * PASSES, 2 * N], U8, name="w_codes", align_bytes=64)
@@ -102,7 +103,7 @@ def tile_moe_tk_lin_gelu_kernel(tc, xT, w_words, w_scales, b, gate, offs, pos1, 
             else:
                 nc.scalar.copy(out=dst, in_=src)
             return lambda: nc.vector.quantize_mx(
-                out=codes[a][:, lo:hi].bitcast(FP8X4),
+                out=(codes[a][:, lo:hi] if a < 2 else late_codes[:, (a - 2) * T + lo:(a - 2) * T + hi]).bitcast(FP8X4),
                 scales=x_scales[4 * a:P, lo:hi],
                 in_=grouped[:].rearrange("p w j -> p (w j)"),
             )
@@ -110,7 +111,7 @@ def tile_moe_tk_lin_gelu_kernel(tc, xT, w_words, w_scales, b, gate, offs, pos1, 
         def gather_codes(a, s0, n):
             nc.vector.tensor_copy(
                 out=slot_codes[a][:, s0:s0 + n],
-                in_=codes[a][:].indirect(offs_t[:, s0 // LIST:(s0 + n) // LIST]),
+                in_=(codes[a][:] if a < 2 else late_codes[:, (a - 2) * T:]).indirect(offs_t[:, s0 // LIST:(s0 + n) // LIST]),
             )
 
         def gather_scales(s0, n):
@@ -128,18 +129,24 @@ def tile_moe_tk_lin_gelu_kernel(tc, xT, w_words, w_scales, b, gate, offs, pos1, 
                     slot_scales[0][4 * a:4 * a + 112, s0:s1].bitcast(I32),
                 )
 
+        waiting = None
         for c0, width in ((0, 256), (256, 256), (512, 256), (768, 128), (896, 128)):
-            quantize(0, c0, c0, c0 + width, True)()
-        for s0 in range(0, S, 768):
+            ready = quantize(0, c0, c0, c0 + width, True)
+            if waiting:
+                waiting()
+            waiting = ready
+        waiting()
+        for s0 in (0, 768, 1536):
             gather_codes(0, s0, 768)
         for c0 in (0, 512):
             quantize(1, c0, c0, c0 + 512, False)()
-        for s0 in (0, 768):
-            gather_codes(1, s0, 768)
+        gather_codes(0, 2304, 768)
+        gather_codes(1, 0, 768)
         for c0 in (0, 512):
             quantize(2, c0, c0, c0 + 512, False)()
         for c0, width in ((0, 512), (512, 256), (768, 256)):
             quantize(3, c0, c0, c0 + width, False)()
+        gather_codes(1, 768, 768)
         gather_and_move_scales(0, 1536)
         gather_and_move_scales(1536, S)
         for r, pos in enumerate((pos1, pos2, pos3)):
@@ -181,7 +188,7 @@ def tile_moe_tk_lin_gelu_kernel(tc, xT, w_words, w_scales, b, gate, offs, pos1, 
                 gather_codes(1, s0, 768)
             gather_codes(2, s0, 768)
             open_groups(s0, s0 + 768)
-            sizes = (768,) if s0 + 768 < S else (640, 128)
+            sizes = (768,) if s0 + 768 < S else (384, 256, 128)
             lo = s0
             for n in sizes:
                 gather_codes(3, lo, n)

@@ -32,15 +32,16 @@ def tile_moe_tk_lin_gelu_kernel(tc, xT, w_words, w_scales, b, gate, offs, pos1, 
     with ExitStack() as ctx:
         keep = ctx.enter_context(tc.tile_pool(name="keep", bufs=1))
         raws = ctx.enter_context(tc.tile_pool(name="raws", bufs=1))
-        stage = ctx.enter_context(tc.tile_pool(name="stage", bufs=4))
+        stage = ctx.enter_context(tc.tile_pool(name="stage", bufs=7))
         prods = ctx.enter_context(tc.tile_pool(name="prods", bufs=1))
         psum = ctx.enter_context(tc.psum_pool(name="psum", bufs=8))
 
         offs_t = keep.tile([P, S // LIST], U16, name="offs_t")
         pos_t = [keep.tile([P, T // LIST], U16, name="pos%d_t" % r) for r in range(TOP)]
         x_scales = keep.tile([P, T], U8, name="x_scales", align_bytes=64)
-        codes = [keep.tile([P, T], U32, name="codes%d" % a, align_bytes=64) for a in range(2)]
-        late_codes = keep.tile([P, 2 * T], U32, name="late_codes", align_bytes=64)
+        first_codes = keep.tile([P, T], U32, name="first_codes", align_bytes=64)
+        late_codes = keep.tile([P, 3 * T], I32, name="late_codes", align_bytes=64)
+        start = {1: T, 2: 0, 3: 2 * T}
         slot_codes = [keep.tile([P, S], U32, name="slot_codes%d" % a, align_bytes=64) for a in range(PASSES)]
         slot_scales = [keep.tile([P, S], U8, name="slot_scales%d" % a, align_bytes=64) for a in range(PASSES)]
         w_codes = keep.tile([P, E * PASSES, 2 * N], U8, name="w_codes", align_bytes=64)
@@ -52,9 +53,10 @@ def tile_moe_tk_lin_gelu_kernel(tc, xT, w_words, w_scales, b, gate, offs, pos1, 
         warm_out = keep.tile([P, 1], F32, name="warm_out")
 
         nc.vector.memset(warm[:], 0.0)
+        nc.vector.memset(late_codes[:, 2 * T:], 0)
         nc.scalar.activation(out=warm_out[:], in_=warm[:], func=AF.Gelu_apprx_tanh)
         nc.gpsimd.memset(x_scales[:].bitcast(I32), 0)
-        nc.vector.memset(w_planes[:].rearrange("p g n -> p (g n)").bitcast(I32), 0)
+        nc.gpsimd.memset(w_planes[:].rearrange("p g n -> p (g n)").bitcast(I32), 0)
         for a in range(1, PASSES):
             nc.vector.memset(slot_scales[a][:].bitcast(I32), 0)
 
@@ -103,7 +105,7 @@ def tile_moe_tk_lin_gelu_kernel(tc, xT, w_words, w_scales, b, gate, offs, pos1, 
             else:
                 nc.scalar.copy(out=dst, in_=src)
             return lambda: nc.vector.quantize_mx(
-                out=(codes[a][:, lo:hi] if a < 2 else late_codes[:, (a - 2) * T + lo:(a - 2) * T + hi]).bitcast(FP8X4),
+                out=(first_codes[:, lo:hi] if a == 0 else late_codes[:, start[a] + lo:start[a] + hi]).bitcast(FP8X4),
                 scales=x_scales[4 * a:P, lo:hi],
                 in_=grouped[:].rearrange("p w j -> p (w j)"),
             )
@@ -111,7 +113,7 @@ def tile_moe_tk_lin_gelu_kernel(tc, xT, w_words, w_scales, b, gate, offs, pos1, 
         def gather_codes(a, s0, n):
             nc.vector.tensor_copy(
                 out=slot_codes[a][:, s0:s0 + n],
-                in_=(codes[a][:] if a < 2 else late_codes[:, (a - 2) * T:]).indirect(offs_t[:, s0 // LIST:(s0 + n) // LIST]),
+                in_=(first_codes[:] if a == 0 else late_codes[:, start[a]:].bitcast(U32)).indirect(offs_t[:, s0 // LIST:(s0 + n) // LIST]),
             )
 
         def gather_scales(s0, n):
@@ -141,12 +143,13 @@ def tile_moe_tk_lin_gelu_kernel(tc, xT, w_words, w_scales, b, gate, offs, pos1, 
         for c0 in (0, 512):
             quantize(1, c0, c0, c0 + 512, False)()
         gather_codes(0, 2304, 768)
-        gather_codes(1, 0, 768)
+        for s0 in (0, 768, 1536):
+            gather_codes(1, s0, 768)
         for c0 in (0, 512):
             quantize(2, c0, c0, c0 + 512, False)()
+        gather_codes(1, 2304, 768)
         for c0, width in ((0, 512), (512, 256), (768, 256)):
             quantize(3, c0, c0, c0 + width, False)()
-        gather_codes(1, 768, 768)
         gather_and_move_scales(0, 1536)
         gather_and_move_scales(1536, S)
         for r, pos in enumerate((pos1, pos2, pos3)):
@@ -184,8 +187,6 @@ def tile_moe_tk_lin_gelu_kernel(tc, xT, w_words, w_scales, b, gate, offs, pos1, 
                 )
 
         for s0 in range(0, S, 768):
-            if s0 >= 1536:
-                gather_codes(1, s0, 768)
             gather_codes(2, s0, 768)
             open_groups(s0, s0 + 768)
             sizes = (768,) if s0 + 768 < S else (384, 256, 128)

from contextlib import ExitStack

import concourse.mybir as mybir

K, T, E, C, N = 2048, 1024, 12, 256, 128
TOP = 3
S = E * C
P = 128
PACK = 4
K_PASS = P * PACK
PASSES = K // K_PASS
FLOPS = 2 * K * N * S

F32 = mybir.dt.float32
BF16 = mybir.dt.bfloat16
I32 = mybir.dt.int32
U32 = mybir.dt.uint32
U16 = mybir.dt.uint16
U8 = mybir.dt.uint8
FP8X4 = mybir.dt.float8_e4m3fn_x4
FP4X4 = mybir.dt.float4_e2m1fn_x4
AF = mybir.ActivationFunctionType
MULT = mybir.AluOpType.mult
ADD = mybir.AluOpType.add

GROUP = 128
LIST = 16


def tile_moe_tk_lin_gelu_kernel(tc, xT, w_words, w_scales, b, gate, offs, pos1, pos2, pos3, out):
    nc = tc.nc
    with ExitStack() as ctx:
        keep = ctx.enter_context(tc.tile_pool(name="keep", bufs=1))
        raws = ctx.enter_context(tc.tile_pool(name="raws", bufs=1))
        stage = ctx.enter_context(tc.tile_pool(name="stage", bufs=7))
        prods = ctx.enter_context(tc.tile_pool(name="prods", bufs=1))
        psum = ctx.enter_context(tc.psum_pool(name="psum", bufs=8))

        offs_t = keep.tile([P, S // LIST], U16, name="offs_t")
        pos_t = [keep.tile([P, T // LIST], U16, name="pos%d_t" % r) for r in range(TOP)]
        x_scales = keep.tile([P, T], U8, name="x_scales", align_bytes=64)
        first_codes = keep.tile([P, T], U32, name="first_codes", align_bytes=64)
        late_codes = keep.tile([P, 3 * T], I32, name="late_codes", align_bytes=64)
        start = {1: T, 2: 0, 3: 2 * T}
        slot_codes = [keep.tile([P, S], U32, name="slot_codes%d" % a, align_bytes=64) for a in range(PASSES)]
        slot_scales = [keep.tile([P, S], U8, name="slot_scales%d" % a, align_bytes=64) for a in range(PASSES)]
        w_codes = keep.tile([P, E * PASSES, 2 * N], U8, name="w_codes", align_bytes=64)
        w_planes = keep.tile([P, E * PASSES, N], U8, name="w_planes", align_bytes=64)
        b_t = keep.tile([P, E], F32, name="b_t")
        gate_t = [keep.tile([P, T], F32, name="gate%d" % r) for r in range(TOP)]
        y = keep.tile([P, S], F32, name="y")
        warm = keep.tile([P, 1], F32, name="warm")
        warm_out = keep.tile([P, 1], F32, name="warm_out")

        nc.vector.memset(warm[:], 0.0)
        nc.vector.memset(late_codes[:, 2 * T:], 0)
        nc.scalar.activation(out=warm_out[:], in_=warm[:], func=AF.Gelu_apprx_tanh)
        nc.gpsimd.memset(x_scales[:].bitcast(I32), 0)
        nc.gpsimd.memset(w_planes[:].rearrange("p g n -> p (g n)").bitcast(I32), 0)
        for a in range(1, PASSES):
            nc.vector.memset(slot_scales[a][:].bitcast(I32), 0)

        def load_x(a, c0, width):
            raw = raws.tile([P, PACK, width], F32, name="raw%d_%d" % (a, c0))
            rows = xT[a * K_PASS:(a + 1) * K_PASS, c0:c0 + width]
            nc.sync.dma_start(raw[:], rows.rearrange("(p j) w -> p j w", j=PACK))
            return raw

        pieces = {}

        def load_pass(a, widths):
            c0 = 0
            for width in widths:
                pieces[(a, c0)] = (load_x(a, c0, width), width)
                c0 += width

        def load_w(e0, e1):
            nc.sync.dma_start(
                w_codes[:, e0 * PASSES:e1 * PASSES, :].bitcast(I32),
                w_words[e0:e1].rearrange("e a p n -> p (e a) n").bitcast(I32),
            )

        load_pass(0, (256, 256, 256, 128, 128))
        nc.sync.dma_start(offs_t[:], offs)
        load_pass(1, (512, 512))
        load_pass(2, (512, 512))
        load_pass(3, (512, 256, 256))
        for r in range(4):
            nc.sync.dma_start(
                w_planes[r:P:32, :, :].bitcast(I32),
                w_scales.rearrange("e a (q r) n -> r q (e a) n", r=4)[r].bitcast(I32),
            )
        for e0 in range(0, E, 3):
            load_w(e0, e0 + 3)
        nc.sync.dma_start(b_t[:], b)

        def quantize(a, key, lo, hi, on_vector):
            raw = pieces[(a, key)][0]
            width = hi - lo
            grouped = stage.tile([P, width, PACK], BF16, name="grouped", align_bytes=64)
            src = raw[:, :, lo - key:hi - key].rearrange("p j (c i) -> p c j i", i=4)
            dst = grouped[:].rearrange("p (c i) j -> p c j i", i=4)
            if on_vector:
                nc.vector.tensor_copy(out=dst, in_=src)
            else:
                nc.scalar.copy(out=dst, in_=src)
            return lambda: nc.vector.quantize_mx(
                out=(first_codes[:, lo:hi] if a == 0 else late_codes[:, start[a] + lo:start[a] + hi]).bitcast(FP8X4),
                scales=x_scales[4 * a:P, lo:hi],
                in_=grouped[:].rearrange("p w j -> p (w j)"),
            )

        def gather_codes(a, s0, n):
            nc.vector.tensor_copy(
                out=slot_codes[a][:, s0:s0 + n],
                in_=(first_codes[:] if a == 0 else late_codes[:, start[a]:].bitcast(U32)).indirect(offs_t[:, s0 // LIST:(s0 + n) // LIST]),
            )

        def gather_scales(s0, n):
            nc.vector.tensor_copy(
                out=slot_scales[0][:, s0:s0 + n],
                in_=x_scales[:].indirect(offs_t[:, s0 // LIST:(s0 + n) // LIST]),
            )

        def gather_and_move_scales(s0, s1):
            for lo in range(s0, s1, 768):
                gather_scales(lo, 768)
            for a in range(1, PASSES):
                nc.sync.dma_start(
                    slot_scales[a][0:112, s0:s1].bitcast(I32),
                    slot_scales[0][4 * a:4 * a + 112, s0:s1].bitcast(I32),
                )

        waiting = None
        for c0, width in ((0, 256), (256, 256), (512, 256), (768, 128), (896, 128)):
            ready = quantize(0, c0, c0, c0 + width, True)
            if waiting:
                waiting()
            waiting = ready
        waiting()
        for s0 in (0, 768, 1536):
            gather_codes(0, s0, 768)
        for c0 in (0, 512):
            quantize(1, c0, c0, c0 + 512, False)()
        gather_codes(0, 2304, 768)
        for s0 in (0, 768, 1536):
            gather_codes(1, s0, 768)
        for c0 in (0, 512):
            quantize(2, c0, c0, c0 + 512, False)()
        gather_codes(1, 2304, 768)
        for c0, width in ((0, 512), (512, 256), (768, 256)):
            quantize(3, c0, c0, c0 + width, False)()
        gather_and_move_scales(0, 1536)
        gather_and_move_scales(1536, S)
        for r, pos in enumerate((pos1, pos2, pos3)):
            nc.sync.dma_start(pos_t[r][:], pos)
            nc.sync.dma_start(gate_t[r][:], gate[r])

        acc = {}

        def multiply(g, a):
            s0, e = g * GROUP, g * GROUP // C
            if a == 0:
                acc[g] = psum.tile([P, GROUP], F32, name="acc")
            nc.tensor.matmul_mx(
                out=acc[g][:],
                lhsT=w_codes[:, e * PASSES + a, :].bitcast(FP4X4),
                lhsT_scale=w_planes[:, e * PASSES + a, :],
                rhs=slot_codes[a][:, s0:s0 + GROUP].bitcast(FP8X4),
                rhs_scale=slot_scales[a][:, s0:s0 + GROUP],
                start=(a == 0),
                stop=(a == PASSES - 1),
            )

        def open_groups(s0, s1):
            for a in range(PASSES - 1):
                for g in range(s0 // GROUP, s1 // GROUP):
                    multiply(g, a)

        def close_groups(s0, s1):
            for g in range(s0 // GROUP, s1 // GROUP):
                multiply(g, PASSES - 1)
                e = g * GROUP // C
                nc.scalar.activation(
                    out=y[:, g * GROUP:(g + 1) * GROUP], in_=acc[g][:],
                    func=AF.Gelu_apprx_tanh, bias=b_t[:, e:e + 1],
                )

        for s0 in range(0, S, 768):
            gather_codes(2, s0, 768)
            open_groups(s0, s0 + 768)
            sizes = (768,) if s0 + 768 < S else (384, 256, 128)
            lo = s0
            for n in sizes:
                gather_codes(3, lo, n)
                close_groups(lo, lo + n)
                lo += n

        prod = [prods.tile([P, T], F32, name="prod%d" % r) for r in range(TOP)]

        def pick(r, t0, t1):
            nc.vector.tensor_tensor(
                prod[r][:, t0:t1], y[:].indirect(pos_t[r][:, t0 // LIST:t1 // LIST]), gate_t[r][:, t0:t1], MULT,
            )

        def add(r, t0, t1):
            nc.vector.tensor_tensor(prod[0][:, t0:t1], prod[0][:, t0:t1], prod[r][:, t0:t1], ADD)

        pick(0, 0, T)
        pick(1, 0, T)
        pick(2, 0, 576)
        add(1, 0, T)
        pick(2, 576, T)
        for t0, t1 in ((0, 576), (576, 800), (800, T)):
            add(2, t0, t1)
            nc.sync.dma_start(out[:, t0:t1], prod[0][:, t0:t1])
